import numpy as np
import ml_dtypes


def mxq(x, axis, fmt="e4m3"):
    dtype, down = {"e4m3": (ml_dtypes.float8_e4m3fn, 7), "e5m2": (ml_dtypes.float8_e5m2, 14)}[fmt]
    v = np.moveaxis(np.asarray(x, np.float32).astype(ml_dtypes.bfloat16).astype(np.float64), axis, -1)
    blocks = v.reshape(v.shape[:-1] + (-1, 32))
    amax = np.abs(blocks).max(-1, keepdims=True)
    byte = np.maximum(np.where(amax > 0, np.frexp(amax)[1] - 1 + 127, 0) - down, 1)
    scale = np.exp2(byte - 127.0)
    codes = (blocks / scale).astype(np.float32).astype(dtype).astype(np.float64)
    return np.moveaxis((codes * scale).reshape(v.shape), -1, axis)


WIDE = False


def mx_kscale(k):
    if not WIDE:
        return np.ones(k)
    levels = np.array([30, -30])
    if k % 512:
        return np.exp2(np.random.permutation(np.resize(levels, k // 32))).repeat(32)
    a = np.empty((k // 512, 16))
    for p in range(k // 512):
        a[p, :8] = np.random.permutation(np.resize(levels, 8))
        for g in range(8):
            far = levels[np.abs(levels - a[p, g]) >= 10]
            a[p, g + 8] = far[np.random.randint(len(far))]
    return np.exp2(a.ravel()).repeat(32)


def f64(x):
    return np.asarray(x).astype(np.float64)


def striped(idx):
    return np.tile(np.asarray(idx).reshape(-1, 16).T, (8, 1)).astype(np.uint16)


def unstriped(offs):
    return offs[:16].T.reshape(-1).astype(np.int64)


E2M1 = np.array([0.0, 0.5, 1.0, 1.5, 2.0, 3.0, 4.0, 6.0, -0.0, -0.5, -1.0, -1.5, -2.0, -3.0, -4.0, -6.0])


def pack_weight(w, fmt):
    k, n = w.shape
    w = f64(np.asarray(w, np.float32).astype(ml_dtypes.bfloat16)).reshape(k // 32, 32, n)
    amax = np.abs(w).max(1)
    if fmt in ("e4m3", "e5m2"):
        byte = np.frexp(amax)[1] - 1 + 127 - (7 if fmt == "e4m3" else 14)
    else:
        mant, ex = np.frexp(amax / 6.0)
        byte = np.where(mant > 0.5, ex, ex - 1) + 127
    byte = np.clip(np.where(amax > 0, byte, 1), 1, 254)
    scaled = (w * np.exp2(127.0 - byte)[:, None, :]).reshape(k, n).astype(np.float32)
    by_word = np.ascontiguousarray(scaled.reshape(k // 512, 128, 4, n).transpose(0, 1, 3, 2))
    if fmt in ("e4m3", "e5m2"):
        words = by_word.astype(ml_dtypes.float8_e4m3fn if fmt == "e4m3" else ml_dtypes.float8_e5m2).view(np.uint8)
    else:
        c = by_word.astype(ml_dtypes.float4_e2m1fn).view(np.uint8) & 0xF
        words = (c[..., 0::2] | (c[..., 1::2] << 4)).reshape(k // 512, 128, 2 * n)
    return np.ascontiguousarray(words), np.ascontiguousarray(byte.astype(np.uint8).reshape(k // 512, 16, n))


def unpack_weight(words, scales, fmt):
    g, _, n = scales.shape
    words = np.ascontiguousarray(words).reshape(g, 128, n, -1)
    if fmt in ("e4m3", "e5m2"):
        vals = words.view(ml_dtypes.float8_e4m3fn if fmt == "e4m3" else ml_dtypes.float8_e5m2).astype(np.float64)
    else:
        nib = np.empty((g, 128, n, 4), np.uint8)
        nib[..., 0::2] = words & 0xF
        nib[..., 1::2] = words >> 4
        vals = E2M1[nib]
    vals = vals * np.repeat(np.exp2(scales.astype(np.float64) - 127.0), 8, axis=1)[..., None]
    return vals.transpose(0, 1, 3, 2).reshape(g * 512, n)


K, T, J, R, N, Z = 1024, 1024, 384, 512, 256, 512


def setup_inputs():
    n = np.random.standard_normal
    idx = np.random.permutation(T)[:J]
    idx2 = np.random.permutation(T)[:J]
    idx3 = np.random.permutation(Z)[:J]
    fk = mx_kscale(K)
    fr = mx_kscale(R)
    wp = pack_weight(n((K, R)) * 1 / np.sqrt(K) * fk[:, None] * fr, "e2m1")
    wbp = pack_weight(n((R, N)) * 1 / np.sqrt(R) / fr[:, None], "e5m2")
    return {
        "xf": (n((K, T))).astype(np.float32),
        "fk": (np.random.uniform(0.5, 2.0, (K, 1)) / fk[:, None]).astype(np.float32),
        "w_words": wp[0],
        "w_scales": wp[1],
        "us": (np.random.uniform(0.5, 2.0, (R, 1)) * fr[:, None]).astype(np.float32),
        "wb_words": wbp[0],
        "wb_scales": wbp[1],
        "tz": (n((N, Z))).astype(np.float32),
        "offs": striped(idx),
        "offs2": striped(idx2),
        "offs3": striped(idx3),
    }


def reference(xf, fk, w_words, w_scales, us, wb_words, wb_scales, tz, offs, offs2, offs3):
    idx = unstriped(offs)
    idx2 = unstriped(offs2)
    idx3 = unstriped(offs3)
    wu = unpack_weight(w_words, w_scales, "e2m1")
    wbu = unpack_weight(wb_words, wb_scales, "e5m2")
    u = np.maximum(f64(xf)[:, idx], f64(xf)[:, idx2]) * f64(fk)
    uq = mxq(u, 0, "e4m3")
    a = wu.T @ uq
    pk1 = np.max(np.abs(a), axis=1, keepdims=True)
    hid = a / pk1 * f64(us)
    hidq = mxq(hid, 0, "e4m3")
    p = wbu.T @ hidq
    y = p * f64(tz)[:, idx3]
    return y

@@ -1,0 +1,226 @@
+from contextlib import ExitStack
+
+import concourse.mybir as mybir
+
+K, T, J, R, N, Z = 1024, 1024, 384, 512, 256, 512
+FLOPS = 2 * K * R * J + 2 * R * N * J
+
+F32 = mybir.dt.float32
+BF16 = mybir.dt.bfloat16
+I32 = mybir.dt.int32
+U32 = mybir.dt.uint32
+U16 = mybir.dt.uint16
+U8 = mybir.dt.uint8
+E4M3 = mybir.dt.float8_e4m3fn_x4
+E5M2 = mybir.dt.float8_e5m2_x4
+E2M1 = mybir.dt.float4_e2m1fn_x4
+MULT = mybir.AluOpType.mult
+MAX = mybir.AluOpType.max
+COPY = mybir.ActivationFunctionType.Copy
+ABS = mybir.ActivationFunctionType.Abs
+AXIS_X = mybir.AxisListType.X
+
+P = 128
+PACK = 4
+PASSES = K // (P * PACK)
+CH = 128
+CHUNKS = J // CH
+HALVES = N // P
+LINE = 4
+VECTOR_PLANES = 3
+WHOLE = 2
+
+
+def tile_list_largerpicks_peakscaled_timeslook_kernel(
+    tc, xf, fk, w_words, w_scales, us, wb_words, wb_scales, tz, offs, offs2, offs3, out
+):
+    nc = tc.nc
+    with ExitStack() as ctx:
+        keep = ctx.enter_context(tc.tile_pool(name="keep", bufs=1))
+        psum = ctx.enter_context(tc.psum_pool(name="psum", bufs=1))
+
+        list_a = keep.tile([P, J // 16], U16)
+        list_b = keep.tile([P, J // 16], U16)
+        list_z = keep.tile([P, J // 16], U16)
+        planes = [keep.tile([P, T], F32, name=f"plane{q}") for q in range(PASSES * PACK)]
+        tables = [keep.tile([P, Z], F32, name=f"table{h}") for h in range(HALVES)]
+        fk_sb = keep.tile([P, PASSES, PACK], F32)
+        us_sb = keep.tile([P, PACK], F32)
+        w_raw = keep.tile([P, PASSES, 2 * R], U8, align_bytes=64)
+        ws_raw = keep.tile([P, PASSES, R], U8, align_bytes=64)
+        w_codes = keep.tile([P, PASSES, 2 * R], U8, align_bytes=64)
+        w_plane = keep.tile([P, PASSES, R], U8, align_bytes=64)
+        wb_codes = keep.tile([P, N], U32, align_bytes=64)
+        wb_plane = keep.tile([P, N], U8, align_bytes=64)
+
+        x_rows = xf.rearrange("(z p t) c -> z t p c", p=P, t=PACK)
+
+        nc.gpsimd.memset(ws_raw[:].bitcast(I32), 0)
+        nc.gpsimd.memset(wb_plane[:].bitcast(I32), 0)
+
+        nc.sync.dma_start(list_a[:], offs)
+        nc.sync.dma_start(list_b[:], offs2)
+        nc.sync.dma_start(planes[0][:], x_rows[0, 0])
+        nc.scalar.dma_start(w_raw[:].bitcast(I32), w_words.rearrange("z p c -> p z c").bitcast(I32))
+        for q in range(4):
+            nc.scalar.dma_start(
+                ws_raw[32 * q : 32 * q + 4].bitcast(I32),
+                w_scales[:, 4 * q : 4 * q + 4, :].rearrange("z r c -> r z c").bitcast(I32),
+            )
+        nc.sync.dma_start(planes[1][:], x_rows[0, 1])
+        nc.sync.dma_start(fk_sb[:], fk.rearrange("(z p t) o -> p z (t o)", p=P, t=PACK))
+        for q in range(2, PASSES * PACK):
+            nc.sync.dma_start(planes[q][:], x_rows[q // PACK, q % PACK])
+        nc.sync.dma_start(list_z[:], offs3)
+        for h in range(HALVES):
+            nc.sync.dma_start(tables[h][:], tz[h * P : (h + 1) * P, :])
+        nc.sync.dma_start(us_sb[:], us.rearrange("(p t) o -> p (t o)", t=PACK))
+        nc.sync.dma_start(wb_codes[:].bitcast(I32), wb_words[0].rearrange("p n t -> p (n t)").bitcast(I32))
+        for q in range(4):
+            nc.sync.dma_start(
+                wb_plane[32 * q : 32 * q + 4].bitcast(I32), wb_scales[0, 4 * q : 4 * q + 4, :].bitcast(I32)
+            )
+
+        nc.vector.tensor_copy(
+            w_codes[:].bitcast(U16).rearrange("p z (t m) -> p z t m", t=PACK),
+            w_raw[:].bitcast(U16).rearrange("p z (m t) -> p z t m", t=PACK),
+        )
+        nc.vector.tensor_copy(
+            w_plane[:].rearrange("p z (t m) -> p z t m", t=PACK),
+            ws_raw[:].rearrange("p z (m t) -> p z t m", t=PACK),
+        )
+
+        def gather(on_vector, dst, window, offsets):
+            if on_vector:
+                nc.vector.tensor_copy(dst, window[:].indirect(offsets))
+            else:
+                nc.scalar.activation(dst, window[:].indirect(offsets), COPY)
+
+        larger = [keep.tile([P, CHUNKS, PACK, CH], F32, name=f"larger{z}") for z in range(PASSES)]
+        a_banks = [psum.tile([P, PACK, CH], F32, name=f"a_bank{c}") for c in range(CHUNKS)]
+
+        def whole_plane(q):
+            pick_a = keep.tile([P, J], F32, name=f"pick_a{q}")
+            pick_b = keep.tile([P, J], F32, name=f"pick_b{q}")
+            gather(False, pick_a[:], planes[q], list_a[:])
+            gather(q < VECTOR_PLANES, pick_b[:], planes[q], list_b[:])
+            nc.vector.tensor_tensor(
+                larger[q // PACK][:, :, q % PACK, :],
+                pick_a[:].rearrange("p (c j) -> p c j", j=CH),
+                pick_b[:].rearrange("p (c j) -> p c j", j=CH),
+                MAX,
+            )
+
+        def chunk_planes(c):
+            z = PASSES - 1
+            pick_a = keep.tile([P, PACK - WHOLE, CH], F32, name=f"part_a{c}")
+            pick_b = keep.tile([P, PACK - WHOLE, CH], F32, name=f"part_b{c}")
+            cols = slice(c * CH // 16, (c + 1) * CH // 16)
+            for t in range(WHOLE, PACK):
+                gather(False, pick_a[:, t - WHOLE, :], planes[z * PACK + t], list_a[:, cols])
+                gather(False, pick_b[:, t - WHOLE, :], planes[z * PACK + t], list_b[:, cols])
+            nc.vector.tensor_tensor(larger[z][:, c, WHOLE:PACK, :], pick_a[:], pick_b[:], MAX)
+
+        u_bf = {}
+        u_codes = {}
+        u_plane = {}
+
+        def weave_u(z, c):
+            u_bf[z, c] = keep.tile([P, CH * PACK], BF16, name=f"u_bf{z}_{c}", align_bytes=64)
+            nc.vector.tensor_tensor(
+                u_bf[z, c][:].rearrange("p (g i t) -> p g t i", i=LINE, t=PACK),
+                larger[z][:, c].rearrange("p t (g i) -> p g t i", i=LINE),
+                fk_sb[:, z, :].unsqueeze(1).unsqueeze(3).to_broadcast([P, CH // LINE, PACK, LINE]),
+                MULT,
+            )
+
+        def first_product(z, c):
+            u_codes[z, c] = keep.tile([P, CH], U32, name=f"u_codes{z}_{c}", align_bytes=64)
+            u_plane[z, c] = keep.tile([P, CH], U8, name=f"u_plane{z}_{c}", align_bytes=64)
+            nc.vector.quantize_mx(out=u_codes[z, c][:].bitcast(E4M3), scales=u_plane[z, c][:], in_=u_bf[z, c][:])
+            for t in range(PACK):
+                nc.tensor.matmul_mx(
+                    out=a_banks[c][:, t, :],
+                    lhsT=w_codes[:, z, 2 * P * t : 2 * P * (t + 1)].bitcast(E2M1),
+                    lhsT_scale=w_plane[:, z, P * t : P * (t + 1)],
+                    rhs=u_codes[z, c][:].bitcast(E4M3),
+                    rhs_scale=u_plane[z, c][:],
+                    start=(z == 0 and t == 0),
+                    stop=(z == PASSES - 1 and t == PACK - 1),
+                )
+
+        sizes = [keep.tile([P, PACK, CH + LINE], F32, name=f"sizes{c}") for c in range(CHUNKS)]
+        peak = keep.tile([P, PACK], F32)
+
+        def peak_so_far(c):
+            nc.scalar.activation(sizes[c][:, :, 0:CH], a_banks[c][:], ABS)
+            dst = peak[:] if c == CHUNKS - 1 else sizes[c + 1][:, :, CH]
+            nc.vector.tensor_reduce(dst, sizes[c][:, :, 0 : CH + min(c, 1)], AXIS_X, MAX)
+
+        for q in range(PACK):
+            whole_plane(q)
+        whole_plane(PACK)
+        for c in range(CHUNKS):
+            weave_u(0, c)
+            if c > 0:
+                first_product(0, c - 1)
+        whole_plane(PACK + 1)
+        first_product(0, CHUNKS - 1)
+        for c in range(CHUNKS):
+            chunk_planes(c)
+            weave_u(1, c)
+            first_product(1, c)
+        for c in range(CHUNKS):
+            peak_so_far(c)
+
+        looked = keep.tile([P, HALVES, J], F32)
+        for h in range(HALVES):
+            gather(False, looked[:, h, :], tables[h], list_z[:])
+
+        inverse = keep.tile([P, PACK], F32)
+        factor = keep.tile([P, PACK], F32)
+        nc.vector.reciprocal(inverse[:], peak[:])
+        nc.vector.tensor_tensor(factor[:], inverse[:], us_sb[:], MULT)
+
+        hid_bf = [keep.tile([P, CH, PACK], BF16, name=f"hid_bf{c}", align_bytes=64) for c in range(CHUNKS)]
+        p_banks = [psum.tile([P, HALVES, CH], F32, name=f"p_bank{c}") for c in range(CHUNKS)]
+        out_rows = out.rearrange("(h p) j -> p h j", p=P)
+
+        def weave_hid(c):
+            nc.vector.tensor_tensor(
+                hid_bf[c][:],
+                a_banks[c][:].rearrange("p t j -> p j t"),
+                factor[:].unsqueeze(1).to_broadcast([P, CH, PACK]),
+                MULT,
+            )
+
+        def second_product(c):
+            codes = keep.tile([P, CH], U32, name=f"hid_codes{c}", align_bytes=64)
+            plane = keep.tile([P, CH], U8, name=f"hid_plane{c}", align_bytes=64)
+            nc.vector.quantize_mx(
+                out=codes[:].bitcast(E4M3), scales=plane[:], in_=hid_bf[c][:].rearrange("p j t -> p (j t)")
+            )
+            for h in range(HALVES):
+                nc.tensor.matmul_mx(
+                    out=p_banks[c][:, h, :],
+                    lhsT=wb_codes[:, P * h : P * (h + 1)].bitcast(E5M2),
+                    lhsT_scale=wb_plane[:, P * h : P * (h + 1)],
+                    rhs=codes[:].bitcast(E4M3),
+                    rhs_scale=plane[:],
+                    start=True,
+                    stop=True,
+                )
+
+        def finish(c):
+            cols = slice(c * CH, (c + 1) * CH)
+            result = keep.tile([P, HALVES, CH], F32, name=f"result{c}")
+            nc.vector.tensor_tensor(result[:], p_banks[c][:], looked[:, :, cols], MULT)
+            nc.sync.dma_start(out_rows[:, :, cols], result[:])
+
+        for step in range(CHUNKS + 2):
+            if step < CHUNKS:
+                weave_hid(step)
+            if 1 <= step <= CHUNKS:
+                second_product(step - 1)
+            if step >= 2:
+                finish(step - 2)

@@ -27,8 +27,6 @@ CH = 128
 CHUNKS = J // CH
 HALVES = N // P
 LINE = 4
-VECTOR_PLANES = 3
-WHOLE = 2
 
 
 def tile_list_largerpicks_peakscaled_timeslook_kernel(
@@ -42,35 +40,52 @@ def tile_list_largerpicks_peakscaled_timeslook_kernel(
         list_a = keep.tile([P, J // 16], U16)
         list_b = keep.tile([P, J // 16], U16)
         list_z = keep.tile([P, J // 16], U16)
-        planes = [keep.tile([P, T], F32, name=f"plane{q}") for q in range(PASSES * PACK)]
+        planes = [keep.tile([P, T], F32, name=f"x_rows{q}") for q in range(PASSES * PACK)]
         tables = [keep.tile([P, Z], F32, name=f"table{h}") for h in range(HALVES)]
         fk_sb = keep.tile([P, PASSES, PACK], F32)
         us_sb = keep.tile([P, PACK], F32)
         w_raw = keep.tile([P, PASSES, 2 * R], U8, align_bytes=64)
-        ws_raw = keep.tile([P, PASSES, R], U8, align_bytes=64)
+        ws_raw = keep.tile([P, R], U8, align_bytes=64)
+        ws_dealt = keep.tile([P, R], U8, align_bytes=64)
         w_codes = keep.tile([P, PASSES, 2 * R], U8, align_bytes=64)
         w_plane = keep.tile([P, PASSES, R], U8, align_bytes=64)
         wb_codes = keep.tile([P, N], U32, align_bytes=64)
         wb_plane = keep.tile([P, N], U8, align_bytes=64)
 
+        a_last = keep.tile([P, PACK, CH + LINE], F32)
+        nc.vector.memset(a_last[:, :, CH + 1 : CH + LINE], 0.0)
         x_rows = xf.rearrange("(z p t) c -> z t p c", p=P, t=PACK)
 
-        nc.gpsimd.memset(ws_raw[:].bitcast(I32), 0)
+        nc.gpsimd.memset(ws_raw[32:64].bitcast(I32), 0)
+        nc.gpsimd.memset(ws_raw[64:128].bitcast(I32), 0)
+        nc.gpsimd.memset(w_plane[:].bitcast(I32), 0)
         nc.gpsimd.memset(wb_plane[:].bitcast(I32), 0)
 
         nc.sync.dma_start(list_a[:], offs)
         nc.sync.dma_start(list_b[:], offs2)
         nc.sync.dma_start(planes[0][:], x_rows[0, 0])
         nc.scalar.dma_start(w_raw[:].bitcast(I32), w_words.rearrange("z p c -> p z c").bitcast(I32))
-        for q in range(4):
-            nc.scalar.dma_start(
-                ws_raw[32 * q : 32 * q + 4].bitcast(I32),
-                w_scales[:, 4 * q : 4 * q + 4, :].rearrange("z r c -> r z c").bitcast(I32),
-            )
+        nc.scalar.dma_start(ws_raw[0:32].bitcast(I32), w_scales.rearrange("z q c -> (z q) c").bitcast(I32))
         nc.sync.dma_start(planes[1][:], x_rows[0, 1])
-        nc.sync.dma_start(fk_sb[:], fk.rearrange("(z p t) o -> p z (t o)", p=P, t=PACK))
         for q in range(2, PASSES * PACK):
             nc.sync.dma_start(planes[q][:], x_rows[q // PACK, q % PACK])
+            if q == 4:
+                nc.sync.dma_start(fk_sb[:], fk.rearrange("(z p t) o -> p z (t o)", p=P, t=PACK))
+        nc.vector.tensor_copy(
+            w_codes[:].bitcast(U16).rearrange("p z (t m) -> p z t m", t=PACK),
+            w_raw[:].bitcast(U16).rearrange("p z (m t) -> p z t m", t=PACK),
+        )
+
+        nc.vector.tensor_copy(
+            ws_dealt[:].rearrange("p (t m) -> p t m", t=PACK), ws_raw[:].rearrange("p (m t) -> p t m", t=PACK)
+        )
+        for z in range(PASSES):
+            for quad in range(4):
+                row = 16 * z + 4 * quad
+                (nc.gpsimd if z == 0 else nc.sync).dma_start(
+                    w_plane[32 * quad : 32 * quad + 4, z, :].bitcast(I32), ws_dealt[row : row + 4].bitcast(I32)
+                )
+
         nc.sync.dma_start(list_z[:], offs3)
         for h in range(HALVES):
             nc.sync.dma_start(tables[h][:], tz[h * P : (h + 1) * P, :])
@@ -81,99 +96,96 @@ def tile_list_largerpicks_peakscaled_timeslook_kernel(
                 wb_plane[32 * q : 32 * q + 4].bitcast(I32), wb_scales[0, 4 * q : 4 * q + 4, :].bitcast(I32)
             )
 
-        nc.vector.tensor_copy(
-            w_codes[:].bitcast(U16).rearrange("p z (t m) -> p z t m", t=PACK),
-            w_raw[:].bitcast(U16).rearrange("p z (m t) -> p z t m", t=PACK),
-        )
-        nc.vector.tensor_copy(
-            w_plane[:].rearrange("p z (t m) -> p z t m", t=PACK),
-            ws_raw[:].rearrange("p z (m t) -> p z t m", t=PACK),
-        )
-
         def gather(on_vector, dst, window, offsets):
             if on_vector:
                 nc.vector.tensor_copy(dst, window[:].indirect(offsets))
             else:
                 nc.scalar.activation(dst, window[:].indirect(offsets), COPY)
 
-        larger = [keep.tile([P, CHUNKS, PACK, CH], F32, name=f"larger{z}") for z in range(PASSES)]
-        a_banks = [psum.tile([P, PACK, CH], F32, name=f"a_bank{c}") for c in range(CHUNKS)]
+        a_banks = [psum.tile([P, PACK, CH], F32, name=f"a_bank{c}") for c in range(CHUNKS - 1)]
+        a_halves = [psum.tile([P, PACK // 2, CH], F32, name=f"a_half{h}") for h in range(2)]
 
-        def whole_plane(q):
-            pick_a = keep.tile([P, J], F32, name=f"pick_a{q}")
-            pick_b = keep.tile([P, J], F32, name=f"pick_b{q}")
-            gather(False, pick_a[:], planes[q], list_a[:])
-            gather(q < VECTOR_PLANES, pick_b[:], planes[q], list_b[:])
+        def multiply(z, c, codes, plane):
+            group = PACK if c < CHUNKS - 1 else PACK // 2
+            for t in range(PACK):
+                nc.tensor.matmul_mx(
+                    out=a_banks[c][:, t, :] if c < CHUNKS - 1 else a_halves[t // 2][:, t % 2, :],
+                    lhsT=w_codes[:, z, 2 * P * t : 2 * P * (t + 1)].bitcast(E2M1),
+                    lhsT_scale=w_plane[:, z, P * t : P * (t + 1)],
+                    rhs=codes.bitcast(E4M3),
+                    rhs_scale=plane,
+                    start=(z == 0 and t % group == 0),
+                    stop=(z == PASSES - 1 and t % group == group - 1),
+                )
+
+        def weave_u(z, woven, larger):
             nc.vector.tensor_tensor(
-                larger[q // PACK][:, :, q % PACK, :],
-                pick_a[:].rearrange("p (c j) -> p c j", j=CH),
-                pick_b[:].rearrange("p (c j) -> p c j", j=CH),
-                MAX,
-            )
-
-        def chunk_planes(c):
-            z = PASSES - 1
-            pick_a = keep.tile([P, PACK - WHOLE, CH], F32, name=f"part_a{c}")
-            pick_b = keep.tile([P, PACK - WHOLE, CH], F32, name=f"part_b{c}")
-            cols = slice(c * CH // 16, (c + 1) * CH // 16)
-            for t in range(WHOLE, PACK):
-                gather(False, pick_a[:, t - WHOLE, :], planes[z * PACK + t], list_a[:, cols])
-                gather(False, pick_b[:, t - WHOLE, :], planes[z * PACK + t], list_b[:, cols])
-            nc.vector.tensor_tensor(larger[z][:, c, WHOLE:PACK, :], pick_a[:], pick_b[:], MAX)
-
-        u_bf = {}
-        u_codes = {}
-        u_plane = {}
-
-        def weave_u(z, c):
-            u_bf[z, c] = keep.tile([P, CH * PACK], BF16, name=f"u_bf{z}_{c}", align_bytes=64)
-            nc.vector.tensor_tensor(
-                u_bf[z, c][:].rearrange("p (g i t) -> p g t i", i=LINE, t=PACK),
-                larger[z][:, c].rearrange("p t (g i) -> p g t i", i=LINE),
-                fk_sb[:, z, :].unsqueeze(1).unsqueeze(3).to_broadcast([P, CH // LINE, PACK, LINE]),
+                woven.rearrange("p (g i t) -> p g t i", i=LINE, t=PACK),
+                larger.rearrange("p t (g i) -> p g t i", i=LINE),
+                fk_sb[:, z, :].unsqueeze(1).unsqueeze(3).to_broadcast([P, larger.shape[2] // LINE, PACK, LINE]),
                 MULT,
             )
 
-        def first_product(z, c):
-            u_codes[z, c] = keep.tile([P, CH], U32, name=f"u_codes{z}_{c}", align_bytes=64)
-            u_plane[z, c] = keep.tile([P, CH], U8, name=f"u_plane{z}_{c}", align_bytes=64)
-            nc.vector.quantize_mx(out=u_codes[z, c][:].bitcast(E4M3), scales=u_plane[z, c][:], in_=u_bf[z, c][:])
-            for t in range(PACK):
-                nc.tensor.matmul_mx(
-                    out=a_banks[c][:, t, :],
-                    lhsT=w_codes[:, z, 2 * P * t : 2 * P * (t + 1)].bitcast(E2M1),
-                    lhsT_scale=w_plane[:, z, P * t : P * (t + 1)],
-                    rhs=u_codes[z, c][:].bitcast(E4M3),
-                    rhs_scale=u_plane[z, c][:],
-                    start=(z == 0 and t == 0),
-                    stop=(z == PASSES - 1 and t == PACK - 1),
-                )
+        def pick_pair(q, b_on_vector):
+            pick_a = keep.tile([P, 2, J], F32, name=f"pick_a{q}")
+            pick_b = keep.tile([P, 2, J], F32, name=f"pick_b{q}")
+            for i in range(2):
+                gather(False, pick_a[:, i, :], planes[q + i], list_a[:])
+                gather(b_on_vector, pick_b[:, i, :], planes[q + i], list_b[:])
+            return pick_a, pick_b
 
-        sizes = [keep.tile([P, PACK, CH + LINE], F32, name=f"sizes{c}") for c in range(CHUNKS)]
-        peak = keep.tile([P, PACK], F32)
-
-        def peak_so_far(c):
-            nc.scalar.activation(sizes[c][:, :, 0:CH], a_banks[c][:], ABS)
-            dst = peak[:] if c == CHUNKS - 1 else sizes[c + 1][:, :, CH]
-            nc.vector.tensor_reduce(dst, sizes[c][:, :, 0 : CH + min(c, 1)], AXIS_X, MAX)
-
-        for q in range(PACK):
-            whole_plane(q)
-        whole_plane(PACK)
+        larger0 = keep.tile([P, PACK, J], F32)
+        for q in range(0, PACK, 2):
+            pick_a, pick_b = pick_pair(q, True)
+            nc.vector.tensor_tensor(larger0[:, q : q + 2, :], pick_a[:], pick_b[:], MAX)
+        woven0 = keep.tile([P, J * PACK], BF16, align_bytes=64)
+        codes0 = keep.tile([P, J], U32, align_bytes=64)
+        plane0 = keep.tile([P, J], U8, align_bytes=64)
+        weave_u(0, woven0[:], larger0[:])
+        pick_a, pick_b = pick_pair(PACK, False)
+        nc.vector.quantize_mx(out=codes0[:].bitcast(E4M3), scales=plane0[:], in_=woven0[:])
         for c in range(CHUNKS):
-            weave_u(0, c)
+            multiply(0, c, codes0[:, c * CH : (c + 1) * CH], plane0[:, c * CH : (c + 1) * CH])
+
+        larger1 = [keep.tile([P, PACK, CH], F32, name=f"larger1_{c}") for c in range(CHUNKS)]
+        for c in range(CHUNKS):
+            cols = slice(c * CH, (c + 1) * CH)
+            nc.vector.tensor_tensor(larger1[c][:, 0:2, :], pick_a[:, :, cols], pick_b[:, :, cols], MAX)
+        woven1 = [keep.tile([P, CH * PACK], BF16, name=f"woven1_{c}", align_bytes=64) for c in range(CHUNKS)]
+
+        def pick_last(c):
+            last_a = keep.tile([P, 2, CH], F32, name=f"last_a{c}")
+            last_b = keep.tile([P, 2, CH], F32, name=f"last_b{c}")
+            cols = slice(c * CH // 16, (c + 1) * CH // 16)
+            for i in range(2):
+                gather(False, last_a[:, i, :], planes[PACK + 2 + i], list_a[:, cols])
+                gather(False, last_b[:, i, :], planes[PACK + 2 + i], list_b[:, cols])
+            nc.vector.tensor_tensor(larger1[c][:, 2:4, :], last_a[:], last_b[:], MAX)
+
+        def close_chunk(c):
+            codes = keep.tile([P, CH], U32, name=f"codes1_{c}", align_bytes=64)
+            plane = keep.tile([P, CH], U8, name=f"plane1_{c}", align_bytes=64)
+            nc.vector.quantize_mx(out=codes[:].bitcast(E4M3), scales=plane[:], in_=woven1[c][:])
+            multiply(1, c, codes[:], plane[:])
+
+        for c in range(CHUNKS):
+            pick_last(c)
             if c > 0:
-                first_product(0, c - 1)
-        whole_plane(PACK + 1)
-        first_product(0, CHUNKS - 1)
-        for c in range(CHUNKS):
-            chunk_planes(c)
-            weave_u(1, c)
-            first_product(1, c)
-        for c in range(CHUNKS):
-            peak_so_far(c)
+                close_chunk(c - 1)
+            weave_u(1, woven1[c][:], larger1[c][:])
+        close_chunk(CHUNKS - 1)
 
-        looked = keep.tile([P, HALVES, J], F32)
+        sizes = keep.tile([P, PACK, J - CH], F32, tag="shared1")
+        peak = keep.tile([P, PACK], F32)
+        for c in range(CHUNKS - 1):
+            nc.scalar.activation(sizes[:, :, c * CH : (c + 1) * CH], a_banks[c][:], ABS)
+        nc.vector.tensor_reduce(a_last[:, :, CH], sizes[:], AXIS_X, MAX)
+        for h in range(2):
+            pair = slice(2 * h, 2 * h + 2)
+            nc.scalar.activation(a_last[:, pair, 0:CH], a_halves[h][:], COPY)
+            nc.vector.tensor_reduce(peak[:, pair], a_last[:, pair, :], AXIS_X, MAX, apply_absolute_value=True)
+
+        looked = keep.tile([P, HALVES, J], F32, tag="shared1")
         for h in range(HALVES):
             gather(False, looked[:, h, :], tables[h], list_z[:])
 
@@ -187,6 +199,14 @@ def tile_list_largerpicks_peakscaled_timeslook_kernel(
         out_rows = out.rearrange("(h p) j -> p h j", p=P)
 
         def weave_hid(c):
+            if c == CHUNKS - 1:
+                nc.vector.tensor_tensor(
+                    hid_bf[c][:].rearrange("p (g i) t -> p g t i", i=LINE),
+                    a_last[:, :, 0:CH].rearrange("p t (g i) -> p g t i", i=LINE),
+                    factor[:].unsqueeze(1).unsqueeze(3).to_broadcast([P, CH // LINE, PACK, LINE]),
+                    MULT,
+                )
+                return
             nc.vector.tensor_tensor(
                 hid_bf[c][:],
                 a_banks[c][:].rearrange("p t j -> p j t"),

@@ -27,6 +27,7 @@ CH = 128
 CHUNKS = J // CH
 HALVES = N // P
 LINE = 4
+VECTOR_PICKS = (0, 1, 3, 4)
 
 
 def tile_list_largerpicks_peakscaled_timeslook_kernel(
@@ -52,8 +53,6 @@ def tile_list_largerpicks_peakscaled_timeslook_kernel(
         wb_codes = keep.tile([P, N], U32, align_bytes=64)
         wb_plane = keep.tile([P, N], U8, align_bytes=64)
 
-        a_last = keep.tile([P, PACK, CH + LINE], F32)
-        nc.vector.memset(a_last[:, :, CH + 1 : CH + LINE], 0.0)
         x_rows = xf.rearrange("(z p t) c -> z t p c", p=P, t=PACK)
 
         nc.gpsimd.memset(ws_raw[32:64].bitcast(I32), 0)
@@ -64,13 +63,14 @@ def tile_list_largerpicks_peakscaled_timeslook_kernel(
         nc.sync.dma_start(list_a[:], offs)
         nc.sync.dma_start(list_b[:], offs2)
         nc.sync.dma_start(planes[0][:], x_rows[0, 0])
+        nc.scalar.dma_start(fk_sb[:], fk.rearrange("(z p t) o -> p z (t o)", p=P, t=PACK))
         nc.scalar.dma_start(w_raw[:].bitcast(I32), w_words.rearrange("z p c -> p z c").bitcast(I32))
         nc.scalar.dma_start(ws_raw[0:32].bitcast(I32), w_scales.rearrange("z q c -> (z q) c").bitcast(I32))
         nc.sync.dma_start(planes[1][:], x_rows[0, 1])
         for q in range(2, PASSES * PACK):
             nc.sync.dma_start(planes[q][:], x_rows[q // PACK, q % PACK])
-            if q == 4:
-                nc.sync.dma_start(fk_sb[:], fk.rearrange("(z p t) o -> p z (t o)", p=P, t=PACK))
+        fk_wide = keep.tile([P, PASSES, PACK, LINE], F32)
+        nc.scalar.activation(fk_wide[:], fk_sb[:].unsqueeze(3).to_broadcast([P, PASSES, PACK, LINE]), COPY)
         nc.vector.tensor_copy(
             w_codes[:].bitcast(U16).rearrange("p z (t m) -> p z t m", t=PACK),
             w_raw[:].bitcast(U16).rearrange("p z (m t) -> p z t m", t=PACK),
@@ -102,47 +102,45 @@ def tile_list_largerpicks_peakscaled_timeslook_kernel(
             else:
                 nc.scalar.activation(dst, window[:].indirect(offsets), COPY)
 
-        a_banks = [psum.tile([P, PACK, CH], F32, name=f"a_bank{c}") for c in range(CHUNKS - 1)]
-        a_halves = [psum.tile([P, PACK // 2, CH], F32, name=f"a_half{h}") for h in range(2)]
+        a_banks = [psum.tile([P, PACK, CH], F32, name=f"a_bank{c}") for c in range(CHUNKS)]
 
         def multiply(z, c, codes, plane):
-            group = PACK if c < CHUNKS - 1 else PACK // 2
             for t in range(PACK):
                 nc.tensor.matmul_mx(
-                    out=a_banks[c][:, t, :] if c < CHUNKS - 1 else a_halves[t // 2][:, t % 2, :],
+                    out=a_banks[c][:, t, :],
                     lhsT=w_codes[:, z, 2 * P * t : 2 * P * (t + 1)].bitcast(E2M1),
                     lhsT_scale=w_plane[:, z, P * t : P * (t + 1)],
                     rhs=codes.bitcast(E4M3),
                     rhs_scale=plane,
-                    start=(z == 0 and t % group == 0),
-                    stop=(z == PASSES - 1 and t % group == group - 1),
+                    start=(z == 0 and t == 0),
+                    stop=(z == PASSES - 1 and t == PACK - 1),
                 )
 
         def weave_u(z, woven, larger):
             nc.vector.tensor_tensor(
                 woven.rearrange("p (g i t) -> p g t i", i=LINE, t=PACK),
                 larger.rearrange("p t (g i) -> p g t i", i=LINE),
-                fk_sb[:, z, :].unsqueeze(1).unsqueeze(3).to_broadcast([P, larger.shape[2] // LINE, PACK, LINE]),
+                fk_wide[:, z].unsqueeze(1).to_broadcast([P, larger.shape[2] // LINE, PACK, LINE]),
                 MULT,
             )
 
-        def pick_pair(q, b_on_vector):
+        def pick_pair(q):
             pick_a = keep.tile([P, 2, J], F32, name=f"pick_a{q}")
             pick_b = keep.tile([P, 2, J], F32, name=f"pick_b{q}")
             for i in range(2):
                 gather(False, pick_a[:, i, :], planes[q + i], list_a[:])
-                gather(b_on_vector, pick_b[:, i, :], planes[q + i], list_b[:])
+                gather(q + i in VECTOR_PICKS, pick_b[:, i, :], planes[q + i], list_b[:])
             return pick_a, pick_b
 
         larger0 = keep.tile([P, PACK, J], F32)
         for q in range(0, PACK, 2):
-            pick_a, pick_b = pick_pair(q, True)
+            pick_a, pick_b = pick_pair(q)
             nc.vector.tensor_tensor(larger0[:, q : q + 2, :], pick_a[:], pick_b[:], MAX)
         woven0 = keep.tile([P, J * PACK], BF16, align_bytes=64)
         codes0 = keep.tile([P, J], U32, align_bytes=64)
         plane0 = keep.tile([P, J], U8, align_bytes=64)
         weave_u(0, woven0[:], larger0[:])
-        pick_a, pick_b = pick_pair(PACK, False)
+        pick_a, pick_b = pick_pair(PACK)
         nc.vector.quantize_mx(out=codes0[:].bitcast(E4M3), scales=plane0[:], in_=woven0[:])
         for c in range(CHUNKS):
             multiply(0, c, codes0[:, c * CH : (c + 1) * CH], plane0[:, c * CH : (c + 1) * CH])
@@ -175,15 +173,16 @@ def tile_list_largerpicks_peakscaled_timeslook_kernel(
             weave_u(1, woven1[c][:], larger1[c][:])
         close_chunk(CHUNKS - 1)
 
-        sizes = keep.tile([P, PACK, J - CH], F32, tag="shared1")
+        sizes = [keep.tile([P, PACK, CH + LINE], F32, name=f"sizes{c}", tag=f"shared{c}") for c in range(CHUNKS)]
         peak = keep.tile([P, PACK], F32)
-        for c in range(CHUNKS - 1):
-            nc.scalar.activation(sizes[:, :, c * CH : (c + 1) * CH], a_banks[c][:], ABS)
-        nc.vector.tensor_reduce(a_last[:, :, CH], sizes[:], AXIS_X, MAX)
-        for h in range(2):
-            pair = slice(2 * h, 2 * h + 2)
-            nc.scalar.activation(a_last[:, pair, 0:CH], a_halves[h][:], COPY)
-            nc.vector.tensor_reduce(peak[:, pair], a_last[:, pair, :], AXIS_X, MAX, apply_absolute_value=True)
+        last = CHUNKS - 1
+        for c in range(CHUNKS):
+            nc.scalar.activation(sizes[c][:, :, 0:CH], a_banks[c][:], ABS)
+            if c < last:
+                nc.vector.tensor_reduce(sizes[last][:, :, CH + c], sizes[c][:, :, 0:CH], AXIS_X, MAX)
+        nc.vector.tensor_reduce(peak[:], sizes[last][:, :, 0 : CH + last], AXIS_X, MAX)
+        a_last = keep.tile([P, CH, PACK], F32)
+        nc.scalar.activation(a_last[:], a_banks[last][:].rearrange("p t j -> p j t"), COPY)
 
         looked = keep.tile([P, HALVES, J], F32, tag="shared1")
         for h in range(HALVES):
@@ -199,12 +198,9 @@ def tile_list_largerpicks_peakscaled_timeslook_kernel(
         out_rows = out.rearrange("(h p) j -> p h j", p=P)
 
         def weave_hid(c):
-            if c == CHUNKS - 1:
-                nc.vector.tensor_tensor(
-                    hid_bf[c][:].rearrange("p (g i) t -> p g t i", i=LINE),
-                    a_last[:, :, 0:CH].rearrange("p t (g i) -> p g t i", i=LINE),
-                    factor[:].unsqueeze(1).unsqueeze(3).to_broadcast([P, CH // LINE, PACK, LINE]),
-                    MULT,
+            if c == last:
+                nc.gpsimd.tensor_tensor(
+                    hid_bf[c][:], a_last[:], factor[:].unsqueeze(1).to_broadcast([P, CH, PACK]), MULT
                 )
                 return
             nc.vector.tensor_tensor(

@@ -151,14 +151,18 @@ def tile_list_largerpicks_peakscaled_timeslook_kernel(
             nc.vector.tensor_tensor(larger1[c][:, 0:2, :], pick_a[:, :, cols], pick_b[:, :, cols], MAX)
         woven1 = [keep.tile([P, CH * PACK], BF16, name=f"woven1_{c}", align_bytes=64) for c in range(CHUNKS)]
 
+        last_a = [keep.tile([P, 2, CH], F32, name=f"last_a{c}") for c in range(CHUNKS)]
+        last_b = [keep.tile([P, 2, CH], F32, name=f"last_b{c}") for c in range(CHUNKS)]
+
+        def pick_part(on_vector, picks, offsets, c, i):
+            gather(on_vector, picks[c][:, i, :], planes[PACK + 2 + i], offsets[:, c * CH // 16 : (c + 1) * CH // 16])
+
         def pick_last(c):
-            last_a = keep.tile([P, 2, CH], F32, name=f"last_a{c}")
-            last_b = keep.tile([P, 2, CH], F32, name=f"last_b{c}")
-            cols = slice(c * CH // 16, (c + 1) * CH // 16)
             for i in range(2):
-                gather(False, last_a[:, i, :], planes[PACK + 2 + i], list_a[:, cols])
-                gather(False, last_b[:, i, :], planes[PACK + 2 + i], list_b[:, cols])
-            nc.vector.tensor_tensor(larger1[c][:, 2:4, :], last_a[:], last_b[:], MAX)
+                pick_part(False, last_a, list_a, c, i)
+                if c < CHUNKS - 1:
+                    pick_part(False, last_b, list_b, c, i)
+            nc.vector.tensor_tensor(larger1[c][:, 2:4, :], last_a[c][:], last_b[c][:], MAX)
 
         def close_chunk(c):
             codes = keep.tile([P, CH], U32, name=f"codes1_{c}", align_bytes=64)
@@ -171,6 +175,8 @@ def tile_list_largerpicks_peakscaled_timeslook_kernel(
             if c > 0:
                 close_chunk(c - 1)
             weave_u(1, woven1[c][:], larger1[c][:])
+            if c < CHUNKS - 1:
+                pick_part(True, last_b, list_b, CHUNKS - 1, c)
         close_chunk(CHUNKS - 1)
 
         sizes = [keep.tile([P, PACK, CH + LINE], F32, name=f"sizes{c}", tag=f"shared{c}") for c in range(CHUNKS)]
@@ -181,8 +187,6 @@ def tile_list_largerpicks_peakscaled_timeslook_kernel(
             if c < last:
                 nc.vector.tensor_reduce(sizes[last][:, :, CH + c], sizes[c][:, :, 0:CH], AXIS_X, MAX)
         nc.vector.tensor_reduce(peak[:], sizes[last][:, :, 0 : CH + last], AXIS_X, MAX)
-        a_last = keep.tile([P, CH, PACK], F32)
-        nc.scalar.activation(a_last[:], a_banks[last][:].rearrange("p t j -> p j t"), COPY)
 
         looked = keep.tile([P, HALVES, J], F32, tag="shared1")
         for h in range(HALVES):
@@ -198,11 +202,6 @@ def tile_list_largerpicks_peakscaled_timeslook_kernel(
         out_rows = out.rearrange("(h p) j -> p h j", p=P)
 
         def weave_hid(c):
-            if c == last:
-                nc.gpsimd.tensor_tensor(
-                    hid_bf[c][:], a_last[:], factor[:].unsqueeze(1).to_broadcast([P, CH, PACK]), MULT
-                )
-                return
             nc.vector.tensor_tensor(
                 hid_bf[c][:],
                 a_banks[c][:].rearrange("p t j -> p j t"),

from contextlib import ExitStack

import concourse.mybir as mybir

K, T, J, R, N, Z = 1024, 1024, 384, 512, 256, 512
FLOPS = 2 * K * R * J + 2 * R * N * J

F32 = mybir.dt.float32
BF16 = mybir.dt.bfloat16
I32 = mybir.dt.int32
U32 = mybir.dt.uint32
U16 = mybir.dt.uint16
U8 = mybir.dt.uint8
E4M3 = mybir.dt.float8_e4m3fn_x4
E5M2 = mybir.dt.float8_e5m2_x4
E2M1 = mybir.dt.float4_e2m1fn_x4
MULT = mybir.AluOpType.mult
MAX = mybir.AluOpType.max
COPY = mybir.ActivationFunctionType.Copy
ABS = mybir.ActivationFunctionType.Abs
AXIS_X = mybir.AxisListType.X

P = 128
PACK = 4
PASSES = K // (P * PACK)
CH = 128
CHUNKS = J // CH
HALVES = N // P
LINE = 4
VECTOR_PICKS = (0, 1, 3, 4)


def tile_list_largerpicks_peakscaled_timeslook_kernel(
    tc, xf, fk, w_words, w_scales, us, wb_words, wb_scales, tz, offs, offs2, offs3, out
):
    nc = tc.nc
    with ExitStack() as ctx:
        keep = ctx.enter_context(tc.tile_pool(name="keep", bufs=1))
        psum = ctx.enter_context(tc.psum_pool(name="psum", bufs=1))

        list_a = keep.tile([P, J // 16], U16)
        list_b = keep.tile([P, J // 16], U16)
        list_z = keep.tile([P, J // 16], U16)
        planes = [keep.tile([P, T], F32, name=f"x_rows{q}") for q in range(PASSES * PACK)]
        tables = [keep.tile([P, Z], F32, name=f"table{h}") for h in range(HALVES)]
        fk_sb = keep.tile([P, PASSES, PACK], F32)
        us_sb = keep.tile([P, PACK], F32)
        w_raw = keep.tile([P, PASSES, 2 * R], U8, align_bytes=64)
        ws_raw = keep.tile([P, R], U8, align_bytes=64)
        ws_dealt = keep.tile([P, R], U8, align_bytes=64)
        w_codes = keep.tile([P, PASSES, 2 * R], U8, align_bytes=64)
        w_plane = keep.tile([P, PASSES, R], U8, align_bytes=64)
        wb_codes = keep.tile([P, N], U32, align_bytes=64)
        wb_plane = keep.tile([P, N], U8, align_bytes=64)

        x_rows = xf.rearrange("(z p t) c -> z t p c", p=P, t=PACK)

        nc.gpsimd.memset(ws_raw[32:64].bitcast(I32), 0)
        nc.gpsimd.memset(ws_raw[64:128].bitcast(I32), 0)
        nc.gpsimd.memset(w_plane[:].bitcast(I32), 0)
        nc.gpsimd.memset(wb_plane[:].bitcast(I32), 0)

        nc.sync.dma_start(list_a[:], offs)
        nc.sync.dma_start(list_b[:], offs2)
        nc.sync.dma_start(planes[0][:], x_rows[0, 0])
        nc.scalar.dma_start(fk_sb[:], fk.rearrange("(z p t) o -> p z (t o)", p=P, t=PACK))
        nc.scalar.dma_start(w_raw[:].bitcast(I32), w_words.rearrange("z p c -> p z c").bitcast(I32))
        nc.scalar.dma_start(ws_raw[0:32].bitcast(I32), w_scales.rearrange("z q c -> (z q) c").bitcast(I32))
        nc.sync.dma_start(planes[1][:], x_rows[0, 1])
        for q in range(2, PASSES * PACK):
            nc.sync.dma_start(planes[q][:], x_rows[q // PACK, q % PACK])
        fk_wide = keep.tile([P, PASSES, PACK, LINE], F32)
        nc.scalar.activation(fk_wide[:], fk_sb[:].unsqueeze(3).to_broadcast([P, PASSES, PACK, LINE]), COPY)
        nc.vector.tensor_copy(
            w_codes[:].bitcast(U16).rearrange("p z (t m) -> p z t m", t=PACK),
            w_raw[:].bitcast(U16).rearrange("p z (m t) -> p z t m", t=PACK),
        )

        nc.vector.tensor_copy(
            ws_dealt[:].rearrange("p (t m) -> p t m", t=PACK), ws_raw[:].rearrange("p (m t) -> p t m", t=PACK)
        )
        for z in range(PASSES):
            for quad in range(4):
                row = 16 * z + 4 * quad
                (nc.gpsimd if z == 0 else nc.sync).dma_start(
                    w_plane[32 * quad : 32 * quad + 4, z, :].bitcast(I32), ws_dealt[row : row + 4].bitcast(I32)
                )

        nc.sync.dma_start(list_z[:], offs3)
        for h in range(HALVES):
            nc.sync.dma_start(tables[h][:], tz[h * P : (h + 1) * P, :])
        nc.sync.dma_start(us_sb[:], us.rearrange("(p t) o -> p (t o)", t=PACK))
        nc.sync.dma_start(wb_codes[:].bitcast(I32), wb_words[0].rearrange("p n t -> p (n t)").bitcast(I32))
        for q in range(4):
            nc.sync.dma_start(
                wb_plane[32 * q : 32 * q + 4].bitcast(I32), wb_scales[0, 4 * q : 4 * q + 4, :].bitcast(I32)
            )

        def gather(on_vector, dst, window, offsets):
            if on_vector:
                nc.vector.tensor_copy(dst, window[:].indirect(offsets))
            else:
                nc.scalar.activation(dst, window[:].indirect(offsets), COPY)

        a_banks = [psum.tile([P, PACK, CH], F32, name=f"a_bank{c}") for c in range(CHUNKS)]

        def multiply(z, c, codes, plane):
            for t in range(PACK):
                nc.tensor.matmul_mx(
                    out=a_banks[c][:, t, :],
                    lhsT=w_codes[:, z, 2 * P * t : 2 * P * (t + 1)].bitcast(E2M1),
                    lhsT_scale=w_plane[:, z, P * t : P * (t + 1)],
                    rhs=codes.bitcast(E4M3),
                    rhs_scale=plane,
                    start=(z == 0 and t == 0),
                    stop=(z == PASSES - 1 and t == PACK - 1),
                )

        def weave_u(z, woven, larger):
            nc.vector.tensor_tensor(
                woven.rearrange("p (g i t) -> p g t i", i=LINE, t=PACK),
                larger.rearrange("p t (g i) -> p g t i", i=LINE),
                fk_wide[:, z].unsqueeze(1).to_broadcast([P, larger.shape[2] // LINE, PACK, LINE]),
                MULT,
            )

        def pick_pair(q):
            pick_a = keep.tile([P, 2, J], F32, name=f"pick_a{q}")
            pick_b = keep.tile([P, 2, J], F32, name=f"pick_b{q}")
            for i in range(2):
                gather(False, pick_a[:, i, :], planes[q + i], list_a[:])
                gather(q + i in VECTOR_PICKS, pick_b[:, i, :], planes[q + i], list_b[:])
            return pick_a, pick_b

        larger0 = keep.tile([P, PACK, J], F32)
        for q in range(0, PACK, 2):
            pick_a, pick_b = pick_pair(q)
            nc.vector.tensor_tensor(larger0[:, q : q + 2, :], pick_a[:], pick_b[:], MAX)
        woven0 = keep.tile([P, J * PACK], BF16, align_bytes=64)
        codes0 = keep.tile([P, J], U32, align_bytes=64)
        plane0 = keep.tile([P, J], U8, align_bytes=64)
        weave_u(0, woven0[:], larger0[:])
        pick_a, pick_b = pick_pair(PACK)
        nc.vector.quantize_mx(out=codes0[:].bitcast(E4M3), scales=plane0[:], in_=woven0[:])
        for c in range(CHUNKS):
            multiply(0, c, codes0[:, c * CH : (c + 1) * CH], plane0[:, c * CH : (c + 1) * CH])

        larger1 = [keep.tile([P, PACK, CH], F32, name=f"larger1_{c}") for c in range(CHUNKS)]
        for c in range(CHUNKS):
            cols = slice(c * CH, (c + 1) * CH)
            nc.vector.tensor_tensor(larger1[c][:, 0:2, :], pick_a[:, :, cols], pick_b[:, :, cols], MAX)
        woven1 = [keep.tile([P, CH * PACK], BF16, name=f"woven1_{c}", align_bytes=64) for c in range(CHUNKS)]

        last_a = [keep.tile([P, 2, CH], F32, name=f"last_a{c}") for c in range(CHUNKS)]
        last_b = [keep.tile([P, 2, CH], F32, name=f"last_b{c}") for c in range(CHUNKS)]

        def pick_part(on_vector, picks, offsets, c, i):
            gather(on_vector, picks[c][:, i, :], planes[PACK + 2 + i], offsets[:, c * CH // 16 : (c + 1) * CH // 16])

        def pick_last(c):
            for i in range(2):
                pick_part(False, last_a, list_a, c, i)
                if c < CHUNKS - 1:
                    pick_part(False, last_b, list_b, c, i)
            nc.vector.tensor_tensor(larger1[c][:, 2:4, :], last_a[c][:], last_b[c][:], MAX)

        def close_chunk(c):
            codes = keep.tile([P, CH], U32, name=f"codes1_{c}", align_bytes=64)
            plane = keep.tile([P, CH], U8, name=f"plane1_{c}", align_bytes=64)
            nc.vector.quantize_mx(out=codes[:].bitcast(E4M3), scales=plane[:], in_=woven1[c][:])
            multiply(1, c, codes[:], plane[:])

        for c in range(CHUNKS):
            pick_last(c)
            if c > 0:
                close_chunk(c - 1)
            weave_u(1, woven1[c][:], larger1[c][:])
            if c < CHUNKS - 1:
                pick_part(True, last_b, list_b, CHUNKS - 1, c)
        close_chunk(CHUNKS - 1)

        sizes = [keep.tile([P, PACK, CH + LINE], F32, name=f"sizes{c}", tag=f"shared{c}") for c in range(CHUNKS)]
        peak = keep.tile([P, PACK], F32)
        last = CHUNKS - 1
        for c in range(CHUNKS):
            nc.scalar.activation(sizes[c][:, :, 0:CH], a_banks[c][:], ABS)
            if c < last:
                nc.vector.tensor_reduce(sizes[last][:, :, CH + c], sizes[c][:, :, 0:CH], AXIS_X, MAX)
        nc.vector.tensor_reduce(peak[:], sizes[last][:, :, 0 : CH + last], AXIS_X, MAX)

        looked = keep.tile([P, HALVES, J], F32, tag="shared1")
        for h in range(HALVES):
            gather(False, looked[:, h, :], tables[h], list_z[:])

        inverse = keep.tile([P, PACK], F32)
        factor = keep.tile([P, PACK], F32)
        nc.vector.reciprocal(inverse[:], peak[:])
        nc.vector.tensor_tensor(factor[:], inverse[:], us_sb[:], MULT)

        hid_bf = [keep.tile([P, CH, PACK], BF16, name=f"hid_bf{c}", align_bytes=64) for c in range(CHUNKS)]
        p_banks = [psum.tile([P, HALVES, CH], F32, name=f"p_bank{c}") for c in range(CHUNKS)]
        out_rows = out.rearrange("(h p) j -> p h j", p=P)

        def weave_hid(c):
            nc.vector.tensor_tensor(
                hid_bf[c][:],
                a_banks[c][:].rearrange("p t j -> p j t"),
                factor[:].unsqueeze(1).to_broadcast([P, CH, PACK]),
                MULT,
            )

        def second_product(c):
            codes = keep.tile([P, CH], U32, name=f"hid_codes{c}", align_bytes=64)
            plane = keep.tile([P, CH], U8, name=f"hid_plane{c}", align_bytes=64)
            nc.vector.quantize_mx(
                out=codes[:].bitcast(E4M3), scales=plane[:], in_=hid_bf[c][:].rearrange("p j t -> p (j t)")
            )
            for h in range(HALVES):
                nc.tensor.matmul_mx(
                    out=p_banks[c][:, h, :],
                    lhsT=wb_codes[:, P * h : P * (h + 1)].bitcast(E5M2),
                    lhsT_scale=wb_plane[:, P * h : P * (h + 1)],
                    rhs=codes[:].bitcast(E4M3),
                    rhs_scale=plane[:],
                    start=True,
                    stop=True,
                )

        def finish(c):
            cols = slice(c * CH, (c + 1) * CH)
            result = keep.tile([P, HALVES, CH], F32, name=f"result{c}")
            nc.vector.tensor_tensor(result[:], p_banks[c][:], looked[:, :, cols], MULT)
            nc.sync.dma_start(out_rows[:, :, cols], result[:])

        for step in range(CHUNKS + 2):
            if step < CHUNKS:
                weave_hid(step)
            if 1 <= step <= CHUNKS:
                second_product(step - 1)
            if step >= 2:
                finish(step - 2)
